import numpy as np, ml_dtypes
CORES = [50,106,114,52,108,116]
N = 6
import mx_ref
NC, ROOT = 128, 5
A = np.float32(0.0125)
BF = ml_dtypes.bfloat16
def cut(t, i, w=512):
    return t[:, w * i:w * i + w]
def tile(rs):
    return np.stack(rs, axis=2).reshape(128, -1).astype(BF)
def pk(c, s, i=0):
    return (np.ascontiguousarray(c[:, 512 * i:512 * i + 512]), mx_ref.live(s[:, 128 * i:128 * i + 128]))
def raw(rng):
    def f(*shape):
        return mx_ref.flush((rng.standard_normal(shape, dtype=np.float32) * np.exp2(rng.integers(-2, 3, shape[:-1] + (1,)))).astype(BF))
    return {"q": f(N, 128, 4 * NC), "k": f(N, 128, 4 * 512), "v": f(N, 128, 512)}
def raw_blocks(rng):
    d = raw(rng)
    for k in ("v",): d[k] = mx_ref.spread(d[k], rng, 4)
    for k in ("q", "k"): d[k] = mx_ref.spread(d[k], rng, 1)
    return d
def raw_wide(rng):
    d = raw(rng)
    for k in ("v",): d[k] = mx_ref.flush((d[k].astype(np.float32) * np.exp2(rng.integers(-8, 9, (N, 1, 1))).astype(np.float32)).astype(BF))
    return d
def raw_sharp(rng):
    d = raw(rng); v = d["q"].astype(np.float32).reshape(N, 128, -1, 4)
    d["q"] = mx_ref.flush((v * np.exp2(rng.integers(-2, 4, (N, 1, v.shape[2], 1))).astype(np.float32)).reshape(d["q"].shape).astype(BF))
    return d
def raw_offset(rng):
    d = raw(rng); v = d["k"].astype(np.float32).reshape(N, 128, -1, 4)
    d["k"] = mx_ref.flush((v + 12 * rng.standard_normal((1, 128, 1, 4), dtype=np.float32)).reshape(d["k"].shape).astype(BF))
    return d
def pack(d, rng):
    o = {"q": d["q"]}
    for m in ("k", "v"):
        t = d[m]; c = np.zeros(t.shape, np.uint8); s = np.zeros((N, 128, t.shape[2] // 4), np.uint8)
        for r in range(N):
            for i in range(t.shape[2] // 512):
                a, b = mx_ref.quantize(cut(t[r], i)); c[r][:, 512 * i:512 * i + 512] = a; s[r][:, 128 * i:128 * i + 128] = mx_ref.plane(b, rng)
        o[m + "c"], o[m + "s"] = c, s
    return o
def setup_inputs(rng):
    return pack(raw(rng), rng)
def setup_inputs_blocks(rng):
    return pack(raw_blocks(rng), rng)
def setup_inputs_offset(rng):
    return pack(raw_offset(rng), rng)
def setup_inputs_sharp(rng):
    return pack(raw_sharp(rng), rng)
def setup_inputs_wide(rng):
    return pack(raw_wide(rng), rng)
def reference(q, kc, ks, vc, vs, own=None):
    ONE = mx_ref.quantize(np.ones((128, 512), BF)); Q = mx_ref.quantize(q[ROOT])
    S = [[mx_ref.matmul(pk(kc[j], ks[j], b), Q) * A for b in range(4)] for j in range(N)]
    lo = np.stack([np.max(s, axis=(0, 1))[None] for s in S]); hi = np.broadcast_to(lo.max(axis=0) + 8, lo.shape).copy()
    c = lo if own is None else own["c"]
    p = np.stack([tile([np.exp(np.maximum(s - c[j], -20).astype(np.float64)).astype(np.float32) for s in S[j]]) for j in range(N)])
    use = p if own is None else own["p"]
    e = np.exp((c - c.max(axis=0)).astype(np.float64))[:, 0]; wlo = np.zeros((N, N, NC), np.float32); whi = np.ones((N, N, NC), np.float32); wlo[ROOT] = e * (1 - 4e-5); whi[ROOT] = e * (1 + 4e-5)
    w = np.zeros((N, N, NC), np.float32); w[ROOT] = e
    if own is not None: w = own["w"]
    num = den = 0
    for j in range(N):
        P = mx_ref.quantize(use[j])
        num = num + w[ROOT][j].astype(np.float64) * mx_ref.matmul(pk(vc[j], vs[j]), P); den = den + w[ROOT][j].astype(np.float64) * mx_ref.matmul(ONE, P)
    o = np.full((N, 128, NC), np.nan, np.float32); o[ROOT] = (num / den).astype(np.float32)
    return {"c": c, "c__lo": lo, "c__hi": hi, "p": p, "w": w, "w__lo": wlo, "w__hi": whi, "o": o}

@@ -1,0 +1,337 @@
+from concourse.bass import DstId, RemoteDMATransfer
+from concourse.mybir import dt, AluOpType, AxisListType, ActivationFunctionType
+
+N = 6
+A = 0.0125
+SLOT = 132
+MSG = 129
+NE_ON = 8
+NE_OFF = 8
+NE_FWD = 8
+NE_C = 8
+NE_RET = 8
+
+SCRATCH = {
+    "qt": ("sbuf", [128, 512], "bfloat16"),
+    "qcb": ("sbuf", [128, 128], "float8_e4m3fn_x4"),
+    "qsb": ("sbuf", [128, 128], "uint8"),
+    "kcb": ("sbuf", [128, 512], "float8_e4m3fn_x4"),
+    "ksb": ("sbuf", [128, 512], "uint8"),
+    "vob": ("sbuf", [128, 256], "float8_e4m3fn_x4"),
+    "vsb": ("sbuf", [128, 256], "uint8"),
+    "one": ("sbuf", [128, 512], "bfloat16"),
+    "o32": ("sbuf", [128, 32], "float32"),
+    "mr": ("sbuf", [128, 8], "float32"),
+    "y": ("sbuf", [128, 32], "float32"),
+    "x": ("sbuf", [128, 32], "float32"),
+    "cb": ("sbuf", [128, 128], "float32"),
+    "t": ("sbuf", [128, 512], "float32"),
+    "pt": ("sbuf", [128, 512], "bfloat16"),
+    "pcb": ("sbuf", [128, 128], "float8_e4m3fn_x4"),
+    "psb": ("sbuf", [128, 128], "uint8"),
+    "st": ("sbuf", [128, SLOT], "float32"),
+    "zw": ("sbuf", [128, 128], "float32"),
+    "ps": ("psum", [128, 4096], "float32"),
+    "relc": ("sbuf", [128, 4], "float32"),
+    "rela": ("sbuf", [128, SLOT], "float32"),
+    "land": ("sbuf", [128, N * SLOT], "float32"),
+    "cland": ("sbuf", [128, 4 * N], "float32"),
+    "nm": ("sbuf", [128, 4], "float32"),
+    "wt": ("sbuf", [128, 32], "float32"),
+    "wtt": ("sbuf", [128, 32], "float32"),
+    "tm": ("sbuf", [128, N * 128], "float32"),
+    "acc": ("sbuf", [128, 128], "float32"),
+    "dn": ("sbuf", [128, 8], "float32"),
+    "rc": ("sbuf", [128, 4], "float32"),
+    "ot": ("sbuf", [128, 128], "float32"),
+    "z": ("sbuf", [128, 128], "float32"),
+}
+SEMAPHORES = ["qarr", "carr", "rcarr", "raarr", "lsent"] + ["arr%d" % i for i in range(N)] + ["l%d" % i for i in range(110)]
+
+
+def _engines(topo, src, dsts, k):
+    m = topo.mask(src, dsts[0])
+    for d in dsts[1:]:
+        m &= topo.mask(src, d)
+    b = [i for i in range(16) if (m >> i) & 1]
+    step = max(1, len(b) // k)
+    out = 0
+    for i in b[::step][:k]:
+        out |= 1 << i
+    return out
+
+
+def _plan(T, topo):
+    cores = list(T.cores)
+    root = cores[T.root]
+    every = range(topo.CHIPS * topo.CORES_PER_CHIP)
+
+    def neighbours(c):
+        return [x for x in every if topo.chip(x) == topo.chip(c) and x != c]
+
+    fwd = {}
+    for d in cores:
+        if d != root and not topo.may_write(root, d):
+            cand = [x for x in neighbours(root) if topo.may_write(x, d)]
+            cand.sort(key=lambda x: (topo.die(x) != topo.die(d), x not in cores, x))
+            fwd[d] = cand[0]
+    rel = {}
+    for s in cores:
+        if s != root and not topo.may_write(s, root):
+            cand = [x for x in neighbours(s) if topo.may_write(x, root)]
+            cand.sort(key=lambda x: (topo.die(x) != topo.die(s), x in cores, x))
+            rel[s] = cand[0]
+    first = [d for d in cores if d != root and d not in fwd]
+    for f in fwd.values():
+        if f not in first:
+            first.append(f)
+    on = [d for d in first if topo.chip(d) == topo.chip(root)]
+    on.sort(key=lambda x: x not in fwd.values())
+    off = [d for d in first if topo.chip(d) != topo.chip(root)]
+    return cores, root, fwd, rel, on, off
+
+
+def _send_q(g, T, topo, src, dsts, k):
+    m = _engines(topo, src, dsts, k)
+    ids = [DstId(rid=topo.addr(d)[0], pnc=topo.addr(d)[1]) for d in dsts]
+    g.remote_dma_fused([RemoteDMATransfer(dst_ids=ids, dma_engine_mask=m, remote_sem=T.sem.qarr,
+                                          srcs=[T.qcb[:].bitcast(dt.uint8)],
+                                          dsts=[T.qcb[:].bitcast(dt.uint8) for _ in dsts])], local_sem=T.sem.lsent)
+    g.remote_dma_fused([RemoteDMATransfer(dst_ids=ids, dma_engine_mask=m, remote_sem=T.sem.qarr,
+                                          srcs=[T.qsb[:]], dsts=[T.qsb[:] for _ in dsts])], local_sem=T.sem.lsent)
+    return 2 * k
+
+
+def _put(g, T, topo, src, dst, out_ap, in_ap, sem, k):
+    rid, pid, _se = topo.addr(dst)
+    g.remote_dma(out_ap, in_ap, sem, T.sem.lsent, pid, rid, _engines(topo, src, [dst], k))
+    return k
+
+
+def rank_program(g, core, T, topo):
+    cores, root, fwd, rel, on, off = _plan(T, topo)
+    rank = T.rank_of(core)
+    mine = [d for d in fwd if fwd[d] == core]
+    served = [s for s in rel if rel[s] == core]
+    if rank is None and not mine and not served:
+        return
+    nq = 2 * NE_FWD if core in fwd else (2 * NE_ON if core in on else 2 * NE_OFF)
+    sent = 0
+
+    if rank is None:
+        if mine:
+            g.wait_ge(T.sem.qarr, nq)
+            sent += _send_q(g, T, topo, core, mine, NE_FWD)
+        for s in served:
+            r = T.rank_of(s)
+            g.wait_ge(T.sem.rcarr, NE_C)
+            sent += _put(g, T, topo, core, root, T.cland[:, 4 * r:4 * r + 1], T.relc[:, 0:1], T.sem.carr, NE_C)
+            g.wait_ge(T.sem.raarr, NE_RET)
+            sent += _put(g, T, topo, core, root, T.land[:, SLOT * r:SLOT * r + MSG], T.rela[:, 0:MSG],
+                         T.sem["arr%d" % r], NE_RET)
+        g.wait_ge(T.sem.lsent, sent)
+        return
+
+    cnt = [0]
+
+    def new():
+        s = T.sem["l%d" % cnt[0]]
+        cnt[0] += 1
+        return s
+
+    pe, dv, ac, sy = g.tensor, g.vector, g.scalar, g.sync
+    MUL, SUB, ADD, MAX = AluOpType.mult, AluOpType.subtract, AluOpType.add, AluOpType.max
+    EXP, COPY = ActivationFunctionType.Exp, ActivationFunctionType.Copy
+    X = AxisListType.X
+    is_root = core == root
+    u8 = dt.uint8
+
+    s_q, s_k, s_v = new(), new(), new()
+    if is_root:
+        sy.dma_start(T.qt[:], T.q[:]).then_inc(s_q, 16)
+        sy.wait_ge(s_q, 16)
+    q2 = sy if is_root else ac
+    sy.dma_start(T.kcb[:].bitcast(u8), T.kc[:]).then_inc(s_k, 16)
+    q2.dma_start(T.ksb[:], T.ks[:]).then_inc(s_k, 16)
+    sy.dma_start(T.vob[:, 0:128].bitcast(u8), T.vc[:]).then_inc(s_v, 16)
+    q2.dma_start(T.vsb[:, 0:128], T.vs[:]).then_inc(s_v, 16)
+
+    s_m, s_one, s_oq, s_qq = new(), new(), new(), new()
+    dv.memset(T.one[:], 0.0).then_inc(s_m, 1)
+    dv.memset(T.o32[:], 1.0).then_inc(s_m, 1)
+    if is_root:
+        dv.memset(T.wt[:], 0.0).then_inc(s_m, 1)
+    else:
+        dv.memset(T.zw[0:N, :], 0.0).then_inc(s_m, 1)
+    ac.wait_ge(s_m, 3)
+    ac.activation(T.one[:], T.one[:], EXP).then_inc(s_one, 1)
+    dv.wait_ge(s_m, 3)
+    if is_root:
+        dv.wait_ge(s_q, 16)
+        dv.quantize_mx(T.qcb[:], T.qsb[:], T.qt[:]).then_inc(s_qq, 1)
+    dv.wait_ge(s_one, 1)
+    dv.quantize_mx(T.vob[:, 128:256], T.vsb[:, 128:256], T.one[:]).then_inc(s_oq, 1)
+
+    if is_root:
+        g.wait_ge(s_qq, 1)
+        if on:
+            sent += _send_q(g, T, topo, core, on, NE_ON)
+        if off:
+            sent += _send_q(g, T, topo, core, off, NE_OFF)
+        pe.wait_ge(s_qq, 1)
+    else:
+        if mine:
+            g.wait_ge(T.sem.qarr, nq)
+            sent += _send_q(g, T, topo, core, mine, NE_FWD)
+        pe.wait_ge(T.sem.qarr, nq)
+
+    s_mt = [new() for _ in range(4)]
+    s_s = [new() for _ in range(4)]
+    pe.wait_ge(s_k, 32)
+    for i in range(4):
+        pe.matmul_mx(T.ps[:, 512 * i:512 * i + 128], T.qcb[:], T.qsb[:], T.kcb[:, 128 * i:128 * i + 128],
+                     T.ksb[:, 128 * i:128 * i + 128], True, True).then_inc(s_mt[i], 1)
+    for b in range(4):
+        pe.matmul_mx(T.ps[:, 512 * (4 + b):512 * (4 + b) + 128], T.kcb[:, 128 * b:128 * b + 128],
+                     T.ksb[:, 128 * b:128 * b + 128], T.qcb[:], T.qsb[:], True, True).then_inc(s_s[b], 1)
+
+    s_r, s_r2, s_y, s_x = new(), new(), new(), new()
+    for i in range(4):
+        dv.wait_ge(s_mt[i], 1)
+        dv.tensor_reduce(T.mr[:, i:i + 1], T.ps[:, 512 * i:512 * i + 128], X, MAX).then_inc(s_r, 1)
+    dv.wait_ge(s_r, 4)
+    dv.tensor_reduce(T.mr[:, 4:5], T.mr[:, 0:4], X, MAX).then_inc(s_r2, 1)
+    dv.wait_ge(s_r2, 1)
+    dv.tensor_scalar(T.y[:], T.o32[:], T.mr[:, 4:5], A, MUL, MUL).then_inc(s_y, 1)
+    dv.wait_ge(s_y, 1)
+    dv.transpose(T.x[:], T.y[:]).then_inc(s_x, 1)
+    s_cb = [new() for _ in range(4)]
+    g.wait_ge(s_x, 1)
+    for a in range(4):
+        g.partition_broadcast(T.cb[:, 32 * a:32 * a + 32], T.x[32 * a:32 * a + 1, :], 128).then_inc(s_cb[a], 1)
+    s_own = new()
+    if is_root:
+        dv.tensor_copy(T.cland[:, 4 * rank:4 * rank + 1], T.y[:, 0:1]).then_inc(s_own, 1)
+    elif core in rel:
+        sent += _put(g, T, topo, core, rel[core], T.relc[:, 0:1], T.y[:, 0:1], T.sem.rcarr, NE_C)
+    else:
+        sent += _put(g, T, topo, core, root, T.cland[:, 4 * rank:4 * rank + 1], T.y[:, 0:1], T.sem.carr, NE_C)
+
+    s_t, s_e, s_pq, s_a, s_st = new(), new(), new(), new(), new()
+    s_sub = [new() for _ in range(4)]
+    s_cl = [new() for _ in range(4)]
+    for b in range(4):
+        ac.wait_ge(s_s[b], 1)
+        ac.activation(T.t[:, b:512:4], T.ps[:, 512 * (4 + b):512 * (4 + b) + 128], COPY, scale=A).then_inc(s_t, 1)
+    dv.wait_ge(s_t, 4)
+    for a in range(4):
+        lo, hi = 128 * a, 128 * a + 128
+        dv.wait_ge(s_cb[a], 1)
+        for b in range(4):
+            dv.tensor_tensor(T.t[:, lo + b:hi:4], T.t[:, lo + b:hi:4], T.cb[:, 32 * a:32 * a + 32], SUB).then_inc(s_sub[a], 1)
+        dv.wait_ge(s_sub[a], 4)
+        dv.tensor_scalar(T.t[:, lo:hi], T.t[:, lo:hi], -20.0, None, MAX).then_inc(s_cl[a], 1)
+        ac.wait_ge(s_cl[a], 1)
+        ac.activation(T.pt[:, lo:hi], T.t[:, lo:hi], EXP).then_inc(s_e, 1)
+    dv.wait_ge(s_e, 4)
+    dv.quantize_mx(T.pcb[:], T.psb[:], T.pt[:]).then_inc(s_pq, 1)
+
+    pe.wait_ge(s_pq, 1)
+    pe.wait_ge(s_v, 32)
+    pe.wait_ge(s_oq, 1)
+    pe.matmul_mx(T.ps[:, 0:130], T.pcb[:], T.psb[:], T.vob[:, 0:130], T.vsb[:, 0:130], True, True).then_inc(s_a, 1)
+    dv.wait_ge(s_a, 1)
+    if is_root:
+        dv.tensor_copy(T.land[:, SLOT * rank:SLOT * rank + MSG], T.ps[:, 0:MSG]).then_inc(s_st, 1)
+    else:
+        dv.tensor_copy(T.st[:, 0:MSG], T.ps[:, 0:MSG]).then_inc(s_st, 1)
+        g.wait_ge(s_st, 1)
+        if core in rel:
+            sent += _put(g, T, topo, core, rel[core], T.rela[:, 0:MSG], T.st[:, 0:MSG], T.sem.raarr, NE_RET)
+        else:
+            sent += _put(g, T, topo, core, root, T.land[:, SLOT * rank:SLOT * rank + MSG], T.st[:, 0:MSG],
+                         T.sem["arr%d" % rank], NE_RET)
+
+    s_out = new()
+    nout = 0
+    if not is_root:
+        sy.wait_ge(s_m, 3)
+        sy.dma_start(T.w[:], T.zw[0:N, :]).then_inc(s_out, 16)
+        nout += 16
+    for a in range(4):
+        sy.wait_ge(s_cb[a], 1)
+    sy.dma_start(T.c[:], T.cb[0:1, :]).then_inc(s_out, 16)
+    sy.wait_ge(s_e, 4)
+    sy.dma_start(T.p[:], T.pt[:]).then_inc(s_out, 16)
+    nout += 32
+
+    if not is_root:
+        sy.wait_ge(s_out, nout)
+        g.wait_ge(T.sem.lsent, sent)
+        return
+
+    s_nm, s_w, s_wt = new(), new(), new()
+    dv.wait_ge(s_own, 1)
+    dv.wait_ge(T.sem.carr, NE_C * (N - 1))
+    dv.tensor_reduce(T.nm[:, 0:1], T.cland[:, 0:4 * N:4], X, MAX, negate=True).then_inc(s_nm, 1)
+    ac.wait_ge(s_nm, 1)
+    ac.wait_ge(s_own, 1)
+    ac.wait_ge(T.sem.carr, NE_C * (N - 1))
+    ac.activation(T.wt[:, 0:N], T.cland[:, 0:4 * N:4], EXP, bias=T.nm[:, 0:1]).then_inc(s_w, 1)
+    ac.wait_ge(s_w, 1)
+    dv.wait_ge(s_w, 1)
+    dv.transpose(T.wtt[:], T.wt[:]).then_inc(s_wt, 1)
+    sy.wait_ge(s_wt, 1)
+    for a in range(4):
+        sy.dma_start(T.w[:, 32 * a:32 * a + 32], T.wtt[32 * a:32 * a + N, :]).then_inc(s_out, 16)
+        nout += 16
+
+    def late(c):
+        return (c != root, topo.chip(c) != topo.chip(root), c in fwd, c in rel)
+    order = sorted(range(N), key=lambda r: late(cores[r]))
+    s_tm = [new() for _ in range(N)]
+    s_dn = [new() for _ in range(N)]
+    s_ac = [new() for _ in range(N)]
+    s_rc, s_f, s_z = new(), new(), new()
+    for k, j in enumerate(order):
+        if j == rank:
+            ac.wait_ge(s_st, 1)
+            dv.wait_ge(s_st, 1)
+        else:
+            ac.wait_ge(T.sem["arr%d" % j], NE_RET)
+            dv.wait_ge(T.sem["arr%d" % j], NE_RET)
+        ac.activation(T.tm[:, 128 * k:128 * k + 128], T.land[:, SLOT * j:SLOT * j + 128], COPY,
+                      scale=T.wt[:, j:j + 1]).then_inc(s_tm[k], 1)
+        lcol = T.land[:, SLOT * j + 128:SLOT * j + 129]
+        if k == 0:
+            dv.tensor_scalar(T.dn[:, 0:1], lcol, T.wt[:, j:j + 1], None, MUL).then_inc(s_dn[0], 1)
+        else:
+            dv.wait_ge(s_dn[k - 1], 1)
+            dv.tensor_scalar(T.dn[:, k:k + 1], lcol, T.wt[:, j:j + 1], T.dn[:, k - 1:k], MUL, ADD).then_inc(s_dn[k], 1)
+        if k == N - 1:
+            dv.wait_ge(s_dn[k], 1)
+            dv.reciprocal(T.rc[:, 0:1], T.dn[:, k:k + 1]).then_inc(s_rc, 1)
+        dv.wait_ge(s_tm[k], 1)
+        if k == 1:
+            dv.tensor_tensor(T.acc[:], T.tm[:, 0:128], T.tm[:, 128:256], ADD).then_inc(s_ac[1], 1)
+        elif k > 1:
+            dv.wait_ge(s_ac[k - 1], 1)
+            dv.tensor_tensor(T.acc[:], T.acc[:], T.tm[:, 128 * k:128 * k + 128], ADD).then_inc(s_ac[k], 1)
+
+    dv.wait_ge(s_ac[N - 1], 1)
+    dv.wait_ge(s_rc, 1)
+    ac.wait_ge(s_ac[N - 1], 1)
+    ac.wait_ge(s_rc, 1)
+    for b in range(2):
+        dv.tensor_scalar(T.ot[:, 32 * b:32 * b + 32], T.acc[:, b:128:4], T.rc[:, 0:1], None, MUL).then_inc(s_f, 1)
+    for b in range(2, 4):
+        ac.activation(T.ot[:, 32 * b:32 * b + 32], T.acc[:, b:128:4], COPY, scale=T.rc[:, 0:1]).then_inc(s_f, 1)
+    dv.wait_ge(s_f, 4)
+    dv.transpose(T.z[:], T.ot[:]).then_inc(s_z, 1)
+    sy.wait_ge(s_z, 1)
+    ac.wait_ge(s_z, 1)
+    for a in range(4):
+        (sy if a < 2 else ac).dma_start(T.o[:, 32 * a:32 * a + 32], T.z[32 * a:32 * a + 32, :]).then_inc(s_out, 16)
+        nout += 16
+    sy.wait_ge(s_out, nout)
+    g.wait_ge(T.sem.lsent, sent)

@@ -1,8 +1,10 @@
+import math
 from concourse.bass import DstId, RemoteDMATransfer
 from concourse.mybir import dt, AluOpType, AxisListType, ActivationFunctionType
 
 N = 6
 A = 0.0125
+FLOOR = math.exp(-20.0)
 SLOT = 132
 MSG = 129
 NE_ON = 8
@@ -44,9 +46,11 @@ SCRATCH = {
     "dn": ("sbuf", [128, 8], "float32"),
     "rc": ("sbuf", [128, 4], "float32"),
     "ot": ("sbuf", [128, 128], "float32"),
+    "osc": ("sbuf", [128, 128], "float32"),
     "z": ("sbuf", [128, 128], "float32"),
 }
-SEMAPHORES = ["qarr", "carr", "rcarr", "raarr", "lsent"] + ["arr%d" % i for i in range(N)] + ["l%d" % i for i in range(110)]
+SEMAPHORES = (["qarr", "qsarr", "carr", "rcarr", "raarr", "lsent"] + ["arr%d" % i for i in range(N)]
+              + ["l%d" % i for i in range(110)])
 
 
 def _engines(topo, src, dsts, k):
@@ -85,20 +89,28 @@ def _plan(T, topo):
     for f in fwd.values():
         if f not in first:
             first.append(f)
+
+    def urgency(x):
+        fed = [d for d in fwd if fwd[d] == x]
+        return 0 if [d for d in fed if d in rel] else (1 if fed else 2)
     on = [d for d in first if topo.chip(d) == topo.chip(root)]
-    on.sort(key=lambda x: x not in fwd.values())
+    on.sort(key=urgency)
     off = [d for d in first if topo.chip(d) != topo.chip(root)]
     return cores, root, fwd, rel, on, off
 
 
-def _send_q(g, T, topo, src, dsts, k):
+def _send_q(g, T, topo, src, dsts, k, arrived=0):
     m = _engines(topo, src, dsts, k)
     ids = [DstId(rid=topo.addr(d)[0], pnc=topo.addr(d)[1]) for d in dsts]
+    if arrived:
+        g.wait_ge(T.sem.qsarr, arrived)
+    g.remote_dma_fused([RemoteDMATransfer(dst_ids=ids, dma_engine_mask=m, remote_sem=T.sem.qsarr,
+                                          srcs=[T.qsb[:]], dsts=[T.qsb[:] for _ in dsts])], local_sem=T.sem.lsent)
+    if arrived:
+        g.wait_ge(T.sem.qarr, arrived)
     g.remote_dma_fused([RemoteDMATransfer(dst_ids=ids, dma_engine_mask=m, remote_sem=T.sem.qarr,
                                           srcs=[T.qcb[:].bitcast(dt.uint8)],
                                           dsts=[T.qcb[:].bitcast(dt.uint8) for _ in dsts])], local_sem=T.sem.lsent)
-    g.remote_dma_fused([RemoteDMATransfer(dst_ids=ids, dma_engine_mask=m, remote_sem=T.sem.qarr,
-                                          srcs=[T.qsb[:]], dsts=[T.qsb[:] for _ in dsts])], local_sem=T.sem.lsent)
     return 2 * k
 
 
@@ -115,13 +127,12 @@ def rank_program(g, core, T, topo):
     served = [s for s in rel if rel[s] == core]
     if rank is None and not mine and not served:
         return
-    nq = 2 * NE_FWD if core in fwd else (2 * NE_ON if core in on else 2 * NE_OFF)
+    nq = NE_FWD if core in fwd else (NE_ON if core in on else NE_OFF)
     sent = 0
 
     if rank is None:
         if mine:
-            g.wait_ge(T.sem.qarr, nq)
-            sent += _send_q(g, T, topo, core, mine, NE_FWD)
+            sent += _send_q(g, T, topo, core, mine, NE_FWD, nq)
         for s in served:
             r = T.rank_of(s)
             g.wait_ge(T.sem.rcarr, NE_C)
@@ -147,43 +158,43 @@ def rank_program(g, core, T, topo):
     u8 = dt.uint8
 
     s_q, s_k, s_v = new(), new(), new()
+    s_m, s_one, s_oq, s_qq = new(), new(), new(), new()
     if is_root:
         sy.dma_start(T.qt[:], T.q[:]).then_inc(s_q, 16)
-        sy.wait_ge(s_q, 16)
-    q2 = sy if is_root else ac
-    sy.dma_start(T.kcb[:].bitcast(u8), T.kc[:]).then_inc(s_k, 16)
-    q2.dma_start(T.ksb[:], T.ks[:]).then_inc(s_k, 16)
-    sy.dma_start(T.vob[:, 0:128].bitcast(u8), T.vc[:]).then_inc(s_v, 16)
-    q2.dma_start(T.vsb[:, 0:128], T.vs[:]).then_inc(s_v, 16)
-
-    s_m, s_one, s_oq, s_qq = new(), new(), new(), new()
     dv.memset(T.one[:], 0.0).then_inc(s_m, 1)
     dv.memset(T.o32[:], 1.0).then_inc(s_m, 1)
     if is_root:
         dv.memset(T.wt[:], 0.0).then_inc(s_m, 1)
     else:
         dv.memset(T.zw[0:N, :], 0.0).then_inc(s_m, 1)
-    ac.wait_ge(s_m, 3)
-    ac.activation(T.one[:], T.one[:], EXP).then_inc(s_one, 1)
     dv.wait_ge(s_m, 3)
     if is_root:
         dv.wait_ge(s_q, 16)
         dv.quantize_mx(T.qcb[:], T.qsb[:], T.qt[:]).then_inc(s_qq, 1)
-    dv.wait_ge(s_one, 1)
-    dv.quantize_mx(T.vob[:, 128:256], T.vsb[:, 128:256], T.one[:]).then_inc(s_oq, 1)
 
     if is_root:
         g.wait_ge(s_qq, 1)
-        if on:
-            sent += _send_q(g, T, topo, core, on, NE_ON)
+        for d in on:
+            sent += _send_q(g, T, topo, core, [d], NE_ON)
         if off:
             sent += _send_q(g, T, topo, core, off, NE_OFF)
         pe.wait_ge(s_qq, 1)
+        sy.wait_ge(T.sem.lsent, sent)
     else:
         if mine:
-            g.wait_ge(T.sem.qarr, nq)
-            sent += _send_q(g, T, topo, core, mine, NE_FWD)
+            sent += _send_q(g, T, topo, core, mine, NE_FWD, nq)
+        pe.wait_ge(T.sem.qsarr, nq)
         pe.wait_ge(T.sem.qarr, nq)
+
+    q2 = sy if is_root else ac
+    sy.dma_start(T.kcb[:].bitcast(u8), T.kc[:]).then_inc(s_k, 16)
+    q2.dma_start(T.ksb[:], T.ks[:]).then_inc(s_k, 16)
+    sy.dma_start(T.vob[:, 0:128].bitcast(u8), T.vc[:]).then_inc(s_v, 16)
+    q2.dma_start(T.vsb[:, 0:128], T.vs[:]).then_inc(s_v, 16)
+    ac.wait_ge(s_m, 3)
+    ac.activation(T.one[:], T.one[:], EXP).then_inc(s_one, 1)
+    dv.wait_ge(s_one, 1)
+    dv.quantize_mx(T.vob[:, 128:256], T.vsb[:, 128:256], T.one[:]).then_inc(s_oq, 1)
 
     s_mt = [new() for _ in range(4)]
     s_s = [new() for _ in range(4)]
@@ -217,23 +228,31 @@ def rank_program(g, core, T, topo):
     else:
         sent += _put(g, T, topo, core, root, T.cland[:, 4 * rank:4 * rank + 1], T.y[:, 0:1], T.sem.carr, NE_C)
 
-    s_t, s_e, s_pq, s_a, s_st = new(), new(), new(), new(), new()
+    s_fl, s_pq, s_a, s_st = new(), new(), new(), new()
+    s_t = [new() for _ in range(4)]
     s_sub = [new() for _ in range(4)]
-    s_cl = [new() for _ in range(4)]
+    s_e = [new() for _ in range(4)]
     for b in range(4):
         ac.wait_ge(s_s[b], 1)
-        ac.activation(T.t[:, b:512:4], T.ps[:, 512 * (4 + b):512 * (4 + b) + 128], COPY, scale=A).then_inc(s_t, 1)
-    dv.wait_ge(s_t, 4)
+        ac.activation(T.t[:, b:512:4], T.ps[:, 512 * (4 + b):512 * (4 + b) + 128], COPY, scale=A).then_inc(s_t[b], 1)
+
+    def floor(a):
+        dv.wait_ge(s_e[a], 1)
+        dv.tensor_scalar(T.pt[:, 128 * a:128 * a + 128], T.pt[:, 128 * a:128 * a + 128], FLOOR, None, MAX).then_inc(s_fl, 1)
+
     for a in range(4):
         lo, hi = 128 * a, 128 * a + 128
         dv.wait_ge(s_cb[a], 1)
         for b in range(4):
+            if a == 0:
+                dv.wait_ge(s_t[b], 1)
             dv.tensor_tensor(T.t[:, lo + b:hi:4], T.t[:, lo + b:hi:4], T.cb[:, 32 * a:32 * a + 32], SUB).then_inc(s_sub[a], 1)
-        dv.wait_ge(s_sub[a], 4)
-        dv.tensor_scalar(T.t[:, lo:hi], T.t[:, lo:hi], -20.0, None, MAX).then_inc(s_cl[a], 1)
-        ac.wait_ge(s_cl[a], 1)
-        ac.activation(T.pt[:, lo:hi], T.t[:, lo:hi], EXP).then_inc(s_e, 1)
-    dv.wait_ge(s_e, 4)
+        ac.wait_ge(s_sub[a], 4)
+        ac.activation(T.pt[:, lo:hi], T.t[:, lo:hi], EXP).then_inc(s_e[a], 1)
+        if a > 0:
+            floor(a - 1)
+    floor(3)
+    dv.wait_ge(s_fl, 4)
     dv.quantize_mx(T.pcb[:], T.psb[:], T.pt[:]).then_inc(s_pq, 1)
 
     pe.wait_ge(s_pq, 1)
@@ -261,7 +280,9 @@ def rank_program(g, core, T, topo):
     for a in range(4):
         sy.wait_ge(s_cb[a], 1)
     sy.dma_start(T.c[:], T.cb[0:1, :]).then_inc(s_out, 16)
-    sy.wait_ge(s_e, 4)
+    sy.wait_ge(s_fl, 4)
+    if not is_root:
+        sy.wait_ge(T.sem.lsent, sent)
     sy.dma_start(T.p[:], T.pt[:]).then_inc(s_out, 16)
     nout += 32
 
@@ -314,20 +335,23 @@ def rank_program(g, core, T, topo):
         dv.wait_ge(s_tm[k], 1)
         if k == 1:
             dv.tensor_tensor(T.acc[:], T.tm[:, 0:128], T.tm[:, 128:256], ADD).then_inc(s_ac[1], 1)
+        elif k == N - 1:
+            dv.wait_ge(s_ac[k - 1], 1)
+            for b in range(4):
+                dv.tensor_tensor(T.ot[:, 32 * b:32 * b + 32], T.acc[:, b:128:4],
+                                 T.tm[:, 128 * k + b:128 * k + 128:4], ADD).then_inc(s_ac[k], 1)
         elif k > 1:
             dv.wait_ge(s_ac[k - 1], 1)
             dv.tensor_tensor(T.acc[:], T.acc[:], T.tm[:, 128 * k:128 * k + 128], ADD).then_inc(s_ac[k], 1)
 
-    dv.wait_ge(s_ac[N - 1], 1)
+    dv.wait_ge(s_ac[N - 1], 4)
     dv.wait_ge(s_rc, 1)
-    ac.wait_ge(s_ac[N - 1], 1)
+    ac.wait_ge(s_ac[N - 1], 4)
     ac.wait_ge(s_rc, 1)
-    for b in range(2):
-        dv.tensor_scalar(T.ot[:, 32 * b:32 * b + 32], T.acc[:, b:128:4], T.rc[:, 0:1], None, MUL).then_inc(s_f, 1)
-    for b in range(2, 4):
-        ac.activation(T.ot[:, 32 * b:32 * b + 32], T.acc[:, b:128:4], COPY, scale=T.rc[:, 0:1]).then_inc(s_f, 1)
-    dv.wait_ge(s_f, 4)
-    dv.transpose(T.z[:], T.ot[:]).then_inc(s_z, 1)
+    dv.tensor_scalar(T.osc[:, 0:64], T.ot[:, 0:64], T.rc[:, 0:1], None, MUL).then_inc(s_f, 1)
+    ac.activation(T.osc[:, 64:128], T.ot[:, 64:128], COPY, scale=T.rc[:, 0:1]).then_inc(s_f, 1)
+    dv.wait_ge(s_f, 2)
+    dv.transpose(T.z[:], T.osc[:]).then_inc(s_z, 1)
     sy.wait_ge(s_z, 1)
     ac.wait_ge(s_z, 1)
     for a in range(4):

@@ -1,17 +1,16 @@
-import math
 from concourse.bass import DstId, RemoteDMATransfer
 from concourse.mybir import dt, AluOpType, AxisListType, ActivationFunctionType
 
 N = 6
 A = 0.0125
-FLOOR = math.exp(-20.0)
+OW = 2
+OP = 4 * OW
 SLOT = 132
 MSG = 129
-NE_ON = 8
-NE_OFF = 8
-NE_FWD = 8
+NE = 8
 NE_C = 8
 NE_RET = 8
+NE_KV = 16
 
 SCRATCH = {
     "qt": ("sbuf", [128, 512], "bfloat16"),
@@ -23,6 +22,8 @@ SCRATCH = {
     "vsb": ("sbuf", [128, 256], "uint8"),
     "one": ("sbuf", [128, 512], "bfloat16"),
     "o32": ("sbuf", [128, 32], "float32"),
+    "m20": ("sbuf", [128, 2], "float32"),
+    "flo": ("sbuf", [128, 2], "bfloat16"),
     "mr": ("sbuf", [128, 8], "float32"),
     "y": ("sbuf", [128, 32], "float32"),
     "x": ("sbuf", [128, 32], "float32"),
@@ -34,8 +35,6 @@ SCRATCH = {
     "st": ("sbuf", [128, SLOT], "float32"),
     "zw": ("sbuf", [128, 128], "float32"),
     "ps": ("psum", [128, 4096], "float32"),
-    "relc": ("sbuf", [128, 4], "float32"),
-    "rela": ("sbuf", [128, SLOT], "float32"),
     "land": ("sbuf", [128, N * SLOT], "float32"),
     "cland": ("sbuf", [128, 4 * N], "float32"),
     "nm": ("sbuf", [128, 4], "float32"),
@@ -49,20 +48,31 @@ SCRATCH = {
     "osc": ("sbuf", [128, 128], "float32"),
     "z": ("sbuf", [128, 128], "float32"),
 }
-SEMAPHORES = (["qarr", "qsarr", "carr", "rcarr", "raarr", "lsent"] + ["arr%d" % i for i in range(N)]
+SEMAPHORES = (["qarr", "qsarr", "oarr", "carr", "karr", "varr", "lsent"] + ["arr%d" % i for i in range(N)]
               + ["l%d" % i for i in range(110)])
 
 
-def _engines(topo, src, dsts, k):
+def _usable(topo, src, dsts):
     m = topo.mask(src, dsts[0])
     for d in dsts[1:]:
         m &= topo.mask(src, d)
-    b = [i for i in range(16) if (m >> i) & 1]
-    step = max(1, len(b) // k)
+    return [i for i in range(16) if (m >> i) & 1]
+
+
+def _bits(eng):
     out = 0
-    for i in b[::step][:k]:
+    for i in eng:
         out |= 1 << i
     return out
+
+
+def _engines(topo, src, dsts, k):
+    b = _usable(topo, src, dsts)
+    return _bits(b[::max(1, len(b) // k)][:k])
+
+
+def _ids(topo, dsts):
+    return [DstId(rid=topo.addr(d)[0], pnc=topo.addr(d)[1]) for d in dsts]
 
 
 def _plan(T, topo):
@@ -77,7 +87,7 @@ def _plan(T, topo):
     for d in cores:
         if d != root and not topo.may_write(root, d):
             cand = [x for x in neighbours(root) if topo.may_write(x, d)]
-            cand.sort(key=lambda x: (topo.die(x) != topo.die(d), x not in cores, x))
+            cand.sort(key=lambda x: (topo.die(x) != topo.die(d), x in cores, x))
             fwd[d] = cand[0]
     rel = {}
     for s in cores:
@@ -99,9 +109,20 @@ def _plan(T, topo):
     return cores, root, fwd, rel, on, off
 
 
-def _send_q(g, T, topo, src, dsts, k, arrived=0):
-    m = _engines(topo, src, dsts, k)
-    ids = [DstId(rid=topo.addr(d)[0], pnc=topo.addr(d)[1]) for d in dsts]
+def _send_one(g, T, topo, dsts, eng):
+    h = len(eng) // 2
+    g.remote_dma_fused([
+        RemoteDMATransfer(dst_ids=_ids(topo, dsts), dma_engine_mask=_bits(eng[:h]), remote_sem=T.sem.oarr,
+                          srcs=[T.vsb[:, 128:128 + OP]], dsts=[T.vsb[:, 128:128 + OP] for _ in dsts]),
+        RemoteDMATransfer(dst_ids=_ids(topo, dsts), dma_engine_mask=_bits(eng[h:]), remote_sem=T.sem.oarr,
+                          srcs=[T.vob[:, 128:128 + OW].bitcast(dt.uint8)],
+                          dsts=[T.vob[:, 128:128 + OW].bitcast(dt.uint8) for _ in dsts])], local_sem=T.sem.lsent)
+    return len(eng)
+
+
+def _send_q(g, T, topo, dsts, eng, arrived=0):
+    m = _bits(eng)
+    ids = _ids(topo, dsts)
     if arrived:
         g.wait_ge(T.sem.qsarr, arrived)
     g.remote_dma_fused([RemoteDMATransfer(dst_ids=ids, dma_engine_mask=m, remote_sem=T.sem.qsarr,
@@ -111,7 +132,7 @@ def _send_q(g, T, topo, src, dsts, k, arrived=0):
     g.remote_dma_fused([RemoteDMATransfer(dst_ids=ids, dma_engine_mask=m, remote_sem=T.sem.qarr,
                                           srcs=[T.qcb[:].bitcast(dt.uint8)],
                                           dsts=[T.qcb[:].bitcast(dt.uint8) for _ in dsts])], local_sem=T.sem.lsent)
-    return 2 * k
+    return 2 * len(eng)
 
 
 def _put(g, T, topo, src, dst, out_ap, in_ap, sem, k):
@@ -123,25 +144,35 @@ def _put(g, T, topo, src, dst, out_ap, in_ap, sem, k):
 def rank_program(g, core, T, topo):
     cores, root, fwd, rel, on, off = _plan(T, topo)
     rank = T.rank_of(core)
-    mine = [d for d in fwd if fwd[d] == core]
-    served = [s for s in rel if rel[s] == core]
-    if rank is None and not mine and not served:
+    mine = []
+    for d in fwd:
+        if fwd[d] == core:
+            mine += [rel[d], d] if d in rel else [d]
+    twin_of = ([s for s in rel if rel[s] == core] + [None])[0]
+    if rank is None and not mine and twin_of is None:
         return
-    nq = NE_FWD if core in fwd else (NE_ON if core in on else NE_OFF)
+    feeds = [fwd[d] for d in fwd]
+    leaf = [d for d in on if d not in feeds]
+    given = leaf + [rel[d] if d in rel else d for d in fwd]
     sent = 0
 
-    if rank is None:
-        if mine:
-            sent += _send_q(g, T, topo, core, mine, NE_FWD, nq)
-        for s in served:
-            r = T.rank_of(s)
-            g.wait_ge(T.sem.rcarr, NE_C)
-            sent += _put(g, T, topo, core, root, T.cland[:, 4 * r:4 * r + 1], T.relc[:, 0:1], T.sem.carr, NE_C)
-            g.wait_ge(T.sem.raarr, NE_RET)
-            sent += _put(g, T, topo, core, root, T.land[:, SLOT * r:SLOT * r + MSG], T.rela[:, 0:MSG],
-                         T.sem["arr%d" % r], NE_RET)
+    def make_one(s_a, s_b):
+        g.vector.memset(T.one[:], 1.0).then_inc(s_a, 1)
+        g.vector.wait_ge(s_a, 1)
+        g.vector.quantize_mx(T.vob[:, 128:256], T.vsb[:, 128:256], T.one[:]).then_inc(s_b, 1)
+
+    if rank is None and twin_of is None:
+        make_one(T.sem.l0, T.sem.l1)
+        eng = _usable(topo, core, mine)[:NE]
+        g.wait_ge(T.sem.l1, 1)
+        sent += _send_one(g, T, topo, [d for d in mine if d in given], eng)
+        for i, d in enumerate(mine):
+            sent += _send_q(g, T, topo, [d], eng, 0 if i else NE)
         g.wait_ge(T.sem.lsent, sent)
         return
+
+    slot = rank if twin_of is None else T.rank_of(twin_of)
+    sends = core != root and core not in rel
 
     cnt = [0]
 
@@ -158,47 +189,69 @@ def rank_program(g, core, T, topo):
     u8 = dt.uint8
 
     s_q, s_k, s_v = new(), new(), new()
-    s_m, s_one, s_oq, s_qq = new(), new(), new(), new()
+    s_m, s_m1, s_one, s_oq, s_qq = new(), new(), new(), new(), new()
+    maker = core not in given
     if is_root:
         sy.dma_start(T.qt[:], T.q[:]).then_inc(s_q, 16)
-    dv.memset(T.one[:], 0.0).then_inc(s_m, 1)
+    if maker:
+        make_one(s_m1, s_oq)
+    dv.memset(T.m20[:], -20.0).then_inc(s_m, 1)
     dv.memset(T.o32[:], 1.0).then_inc(s_m, 1)
     if is_root:
         dv.memset(T.wt[:], 0.0).then_inc(s_m, 1)
     else:
         dv.memset(T.zw[0:N, :], 0.0).then_inc(s_m, 1)
+
+    if twin_of is not None:
+        kw, vw = [(T.sem.karr, 3 * NE_KV)], [(T.sem.varr, 2 * NE_KV)]
+    elif core in rel:
+        pcs = [(sy, T.vsb[:, 0:128], T.vs[:], 0), (ac, T.ksb[:], T.ks[:], 1),
+               (sy, T.kcb[:, 0:256].bitcast(u8), T.kc[:, 0:1024], 1),
+               (ac, T.kcb[:, 256:512].bitcast(u8), T.kc[:, 1024:2048], 1),
+               (sy, T.vob[:, 0:128].bitcast(u8), T.vc[:], 0)]
+        kw, vw = [], []
+        for qu, buf, src, is_k in pcs:
+            s_p = new()
+            qu.dma_start(buf, src).then_inc(s_p, 16)
+            (kw if is_k else vw).append((s_p, 16))
+            g.wait_ge(s_p, 16)
+            sent += _put(g, T, topo, core, rel[core], buf, buf, T.sem.karr if is_k else T.sem.varr, NE_KV)
+    else:
+        sy.dma_start(T.kcb[:].bitcast(u8), T.kc[:]).then_inc(s_k, 16)
+        ac.dma_start(T.ksb[:], T.ks[:]).then_inc(s_k, 16)
+        sy.dma_start(T.vob[:, 0:128].bitcast(u8), T.vc[:]).then_inc(s_v, 16)
+        ac.dma_start(T.vsb[:, 0:128], T.vs[:]).then_inc(s_v, 16)
+        kw, vw = [(s_k, 32)], [(s_v, 32)]
     dv.wait_ge(s_m, 3)
     if is_root:
         dv.wait_ge(s_q, 16)
         dv.quantize_mx(T.qcb[:], T.qsb[:], T.qt[:]).then_inc(s_qq, 1)
 
     if is_root:
+        off_e = _usable(topo, core, off)[:NE]
+        rest = [e for e in _usable(topo, core, on) if e not in off_e]
+        on_e = (rest if len(rest) >= NE else _usable(topo, core, on))[:NE]
+        g.wait_ge(s_oq, 1)
+        sent += _send_one(g, T, topo, leaf, on_e)
         g.wait_ge(s_qq, 1)
         for d in on:
-            sent += _send_q(g, T, topo, core, [d], NE_ON)
-        if off:
-            sent += _send_q(g, T, topo, core, off, NE_OFF)
+            if d in feeds:
+                sent += _send_q(g, T, topo, [d], on_e)
+        sent += _send_q(g, T, topo, off, off_e)
+        sent += _send_q(g, T, topo, leaf, on_e)
         pe.wait_ge(s_qq, 1)
-        sy.wait_ge(T.sem.lsent, sent)
     else:
-        if mine:
-            sent += _send_q(g, T, topo, core, mine, NE_FWD, nq)
-        pe.wait_ge(T.sem.qsarr, nq)
-        pe.wait_ge(T.sem.qarr, nq)
+        pe.wait_ge(T.sem.qsarr, NE)
+        pe.wait_ge(T.sem.qarr, NE)
 
-    q2 = sy if is_root else ac
-    sy.dma_start(T.kcb[:].bitcast(u8), T.kc[:]).then_inc(s_k, 16)
-    q2.dma_start(T.ksb[:], T.ks[:]).then_inc(s_k, 16)
-    sy.dma_start(T.vob[:, 0:128].bitcast(u8), T.vc[:]).then_inc(s_v, 16)
-    q2.dma_start(T.vsb[:, 0:128], T.vs[:]).then_inc(s_v, 16)
     ac.wait_ge(s_m, 3)
-    ac.activation(T.one[:], T.one[:], EXP).then_inc(s_one, 1)
+    ac.activation(T.flo[:], T.m20[:], EXP).then_inc(s_one, 1)
     dv.wait_ge(s_one, 1)
-    dv.quantize_mx(T.vob[:, 128:256], T.vsb[:, 128:256], T.one[:]).then_inc(s_oq, 1)
 
     s_mt = [new() for _ in range(4)]
     s_s = [new() for _ in range(4)]
-    pe.wait_ge(s_k, 32)
+    for s_p, n_p in kw:
+        pe.wait_ge(s_p, n_p)
     for i in range(4):
         pe.matmul_mx(T.ps[:, 512 * i:512 * i + 128], T.qcb[:], T.qsb[:], T.kcb[:, 128 * i:128 * i + 128],
                      T.ksb[:, 128 * i:128 * i + 128], True, True).then_inc(s_mt[i], 1)
@@ -223,10 +276,8 @@ def rank_program(g, core, T, topo):
     s_own = new()
     if is_root:
         dv.tensor_copy(T.cland[:, 4 * rank:4 * rank + 1], T.y[:, 0:1]).then_inc(s_own, 1)
-    elif core in rel:
-        sent += _put(g, T, topo, core, rel[core], T.relc[:, 0:1], T.y[:, 0:1], T.sem.rcarr, NE_C)
-    else:
-        sent += _put(g, T, topo, core, root, T.cland[:, 4 * rank:4 * rank + 1], T.y[:, 0:1], T.sem.carr, NE_C)
+    elif sends:
+        sent += _put(g, T, topo, core, root, T.cland[:, 4 * slot:4 * slot + 1], T.y[:, 0:1], T.sem.carr, NE_C)
 
     s_fl, s_pq, s_a, s_st = new(), new(), new(), new()
     s_t = [new() for _ in range(4)]
@@ -238,7 +289,8 @@ def rank_program(g, core, T, topo):
 
     def floor(a):
         dv.wait_ge(s_e[a], 1)
-        dv.tensor_scalar(T.pt[:, 128 * a:128 * a + 128], T.pt[:, 128 * a:128 * a + 128], FLOOR, None, MAX).then_inc(s_fl, 1)
+        dv.tensor_scalar(T.pt[:, 128 * a:128 * a + 128], T.pt[:, 128 * a:128 * a + 128], T.flo[:, 0:1], None,
+                         MAX).then_inc(s_fl, 1)
 
     for a in range(4):
         lo, hi = 128 * a, 128 * a + 128
@@ -256,20 +308,25 @@ def rank_program(g, core, T, topo):
     dv.quantize_mx(T.pcb[:], T.psb[:], T.pt[:]).then_inc(s_pq, 1)
 
     pe.wait_ge(s_pq, 1)
-    pe.wait_ge(s_v, 32)
-    pe.wait_ge(s_oq, 1)
-    pe.matmul_mx(T.ps[:, 0:130], T.pcb[:], T.psb[:], T.vob[:, 0:130], T.vsb[:, 0:130], True, True).then_inc(s_a, 1)
+    for s_p, n_p in vw:
+        pe.wait_ge(s_p, n_p)
+    if maker:
+        pe.wait_ge(s_oq, 1)
+    else:
+        pe.wait_ge(T.sem.oarr, NE)
+    pe.matmul_mx(T.ps[:, 0:128 + OW], T.pcb[:], T.psb[:], T.vob[:, 0:128 + OW], T.vsb[:, 0:128 + OW], True,
+                 True).then_inc(s_a, 1)
     dv.wait_ge(s_a, 1)
     if is_root:
         dv.tensor_copy(T.land[:, SLOT * rank:SLOT * rank + MSG], T.ps[:, 0:MSG]).then_inc(s_st, 1)
-    else:
+    elif sends:
         dv.tensor_copy(T.st[:, 0:MSG], T.ps[:, 0:MSG]).then_inc(s_st, 1)
         g.wait_ge(s_st, 1)
-        if core in rel:
-            sent += _put(g, T, topo, core, rel[core], T.rela[:, 0:MSG], T.st[:, 0:MSG], T.sem.raarr, NE_RET)
-        else:
-            sent += _put(g, T, topo, core, root, T.land[:, SLOT * rank:SLOT * rank + MSG], T.st[:, 0:MSG],
-                         T.sem["arr%d" % rank], NE_RET)
+        sent += _put(g, T, topo, core, root, T.land[:, SLOT * slot:SLOT * slot + MSG], T.st[:, 0:MSG],
+                     T.sem["arr%d" % slot], NE_RET)
+    if rank is None:
+        g.wait_ge(T.sem.lsent, sent)
+        return
 
     s_out = new()
     nout = 0

from concourse.bass import DstId, RemoteDMATransfer
from concourse.mybir import dt, AluOpType, AxisListType, ActivationFunctionType

N = 6
A = 0.0125
OW = 2
OP = 4 * OW
SLOT = 132
MSG = 129
NE = 8
NE_C = 8
NE_RET = 8
NE_KV = 16

SCRATCH = {
    "qt": ("sbuf", [128, 512], "bfloat16"),
    "qcb": ("sbuf", [128, 128], "float8_e4m3fn_x4"),
    "qsb": ("sbuf", [128, 128], "uint8"),
    "kcb": ("sbuf", [128, 512], "float8_e4m3fn_x4"),
    "ksb": ("sbuf", [128, 512], "uint8"),
    "vob": ("sbuf", [128, 256], "float8_e4m3fn_x4"),
    "vsb": ("sbuf", [128, 256], "uint8"),
    "one": ("sbuf", [128, 512], "bfloat16"),
    "o32": ("sbuf", [128, 32], "float32"),
    "m20": ("sbuf", [128, 2], "float32"),
    "flo": ("sbuf", [128, 2], "bfloat16"),
    "mr": ("sbuf", [128, 8], "float32"),
    "y": ("sbuf", [128, 32], "float32"),
    "x": ("sbuf", [128, 32], "float32"),
    "cb": ("sbuf", [128, 128], "float32"),
    "t": ("sbuf", [128, 512], "float32"),
    "pt": ("sbuf", [128, 512], "bfloat16"),
    "pcb": ("sbuf", [128, 128], "float8_e4m3fn_x4"),
    "psb": ("sbuf", [128, 128], "uint8"),
    "st": ("sbuf", [128, SLOT], "float32"),
    "zw": ("sbuf", [128, 128], "float32"),
    "ps": ("psum", [128, 4096], "float32"),
    "land": ("sbuf", [128, N * SLOT], "float32"),
    "cland": ("sbuf", [128, 4 * N], "float32"),
    "nm": ("sbuf", [128, 4], "float32"),
    "wt": ("sbuf", [128, 32], "float32"),
    "wtt": ("sbuf", [128, 32], "float32"),
    "tm": ("sbuf", [128, N * 128], "float32"),
    "acc": ("sbuf", [128, 128], "float32"),
    "dn": ("sbuf", [128, 8], "float32"),
    "rc": ("sbuf", [128, 4], "float32"),
    "ot": ("sbuf", [128, 128], "float32"),
    "osc": ("sbuf", [128, 128], "float32"),
    "z": ("sbuf", [128, 128], "float32"),
}
SEMAPHORES = (["qarr", "qsarr", "oarr", "carr", "karr", "varr", "lsent"] + ["arr%d" % i for i in range(N)]
              + ["l%d" % i for i in range(110)])


def _usable(topo, src, dsts):
    m = topo.mask(src, dsts[0])
    for d in dsts[1:]:
        m &= topo.mask(src, d)
    return [i for i in range(16) if (m >> i) & 1]


def _bits(eng):
    out = 0
    for i in eng:
        out |= 1 << i
    return out


def _engines(topo, src, dsts, k):
    b = _usable(topo, src, dsts)
    return _bits(b[::max(1, len(b) // k)][:k])


def _ids(topo, dsts):
    return [DstId(rid=topo.addr(d)[0], pnc=topo.addr(d)[1]) for d in dsts]


def _plan(T, topo):
    cores = list(T.cores)
    root = cores[T.root]
    every = range(topo.CHIPS * topo.CORES_PER_CHIP)

    def neighbours(c):
        return [x for x in every if topo.chip(x) == topo.chip(c) and x != c]

    fwd = {}
    for d in cores:
        if d != root and not topo.may_write(root, d):
            cand = [x for x in neighbours(root) if topo.may_write(x, d)]
            cand.sort(key=lambda x: (topo.die(x) != topo.die(d), x in cores, x))
            fwd[d] = cand[0]
    rel = {}
    for s in cores:
        if s != root and not topo.may_write(s, root):
            cand = [x for x in neighbours(s) if topo.may_write(x, root)]
            cand.sort(key=lambda x: (topo.die(x) != topo.die(s), x in cores, x))
            rel[s] = cand[0]
    first = [d for d in cores if d != root and d not in fwd]
    for f in fwd.values():
        if f not in first:
            first.append(f)

    def urgency(x):
        fed = [d for d in fwd if fwd[d] == x]
        return 0 if [d for d in fed if d in rel] else (1 if fed else 2)
    on = [d for d in first if topo.chip(d) == topo.chip(root)]
    on.sort(key=urgency)
    off = [d for d in first if topo.chip(d) != topo.chip(root)]
    return cores, root, fwd, rel, on, off


def _send_one(g, T, topo, dsts, eng):
    h = len(eng) // 2
    g.remote_dma_fused([
        RemoteDMATransfer(dst_ids=_ids(topo, dsts), dma_engine_mask=_bits(eng[:h]), remote_sem=T.sem.oarr,
                          srcs=[T.vsb[:, 128:128 + OP]], dsts=[T.vsb[:, 128:128 + OP] for _ in dsts]),
        RemoteDMATransfer(dst_ids=_ids(topo, dsts), dma_engine_mask=_bits(eng[h:]), remote_sem=T.sem.oarr,
                          srcs=[T.vob[:, 128:128 + OW].bitcast(dt.uint8)],
                          dsts=[T.vob[:, 128:128 + OW].bitcast(dt.uint8) for _ in dsts])], local_sem=T.sem.lsent)
    return len(eng)


def _send_q(g, T, topo, dsts, eng, arrived=0):
    m = _bits(eng)
    ids = _ids(topo, dsts)
    if arrived:
        g.wait_ge(T.sem.qsarr, arrived)
    g.remote_dma_fused([RemoteDMATransfer(dst_ids=ids, dma_engine_mask=m, remote_sem=T.sem.qsarr,
                                          srcs=[T.qsb[:]], dsts=[T.qsb[:] for _ in dsts])], local_sem=T.sem.lsent)
    if arrived:
        g.wait_ge(T.sem.qarr, arrived)
    g.remote_dma_fused([RemoteDMATransfer(dst_ids=ids, dma_engine_mask=m, remote_sem=T.sem.qarr,
                                          srcs=[T.qcb[:].bitcast(dt.uint8)],
                                          dsts=[T.qcb[:].bitcast(dt.uint8) for _ in dsts])], local_sem=T.sem.lsent)
    return 2 * len(eng)


def _put(g, T, topo, src, dst, out_ap, in_ap, sem, k):
    rid, pid, _se = topo.addr(dst)
    g.remote_dma(out_ap, in_ap, sem, T.sem.lsent, pid, rid, _engines(topo, src, [dst], k))
    return k


def rank_program(g, core, T, topo):
    cores, root, fwd, rel, on, off = _plan(T, topo)
    rank = T.rank_of(core)
    mine = []
    for d in fwd:
        if fwd[d] == core:
            mine += [rel[d], d] if d in rel else [d]
    twin_of = ([s for s in rel if rel[s] == core] + [None])[0]
    if rank is None and not mine and twin_of is None:
        return
    feeds = [fwd[d] for d in fwd]
    leaf = [d for d in on if d not in feeds]
    given = leaf + [rel[d] if d in rel else d for d in fwd]
    sent = 0

    def make_one(s_a, s_b):
        g.vector.memset(T.one[:], 1.0).then_inc(s_a, 1)
        g.vector.wait_ge(s_a, 1)
        g.vector.quantize_mx(T.vob[:, 128:256], T.vsb[:, 128:256], T.one[:]).then_inc(s_b, 1)

    if rank is None and twin_of is None:
        make_one(T.sem.l0, T.sem.l1)
        eng = _usable(topo, core, mine)[:NE]
        g.wait_ge(T.sem.l1, 1)
        sent += _send_one(g, T, topo, [d for d in mine if d in given], eng)
        for i, d in enumerate(mine):
            sent += _send_q(g, T, topo, [d], eng, 0 if i else NE)
        g.wait_ge(T.sem.lsent, sent)
        return

    slot = rank if twin_of is None else T.rank_of(twin_of)
    sends = core != root and core not in rel

    cnt = [0]

    def new():
        s = T.sem["l%d" % cnt[0]]
        cnt[0] += 1
        return s

    pe, dv, ac, sy = g.tensor, g.vector, g.scalar, g.sync
    MUL, SUB, ADD, MAX = AluOpType.mult, AluOpType.subtract, AluOpType.add, AluOpType.max
    EXP, COPY = ActivationFunctionType.Exp, ActivationFunctionType.Copy
    X = AxisListType.X
    is_root = core == root
    u8 = dt.uint8

    s_q, s_k, s_v = new(), new(), new()
    s_m, s_m1, s_one, s_oq, s_qq = new(), new(), new(), new(), new()
    maker = core not in given
    if is_root:
        sy.dma_start(T.qt[:], T.q[:]).then_inc(s_q, 16)
    if maker:
        make_one(s_m1, s_oq)
    dv.memset(T.m20[:], -20.0).then_inc(s_m, 1)
    dv.memset(T.o32[:], 1.0).then_inc(s_m, 1)
    if is_root:
        dv.memset(T.wt[:], 0.0).then_inc(s_m, 1)
    else:
        dv.memset(T.zw[0:N, :], 0.0).then_inc(s_m, 1)

    if twin_of is not None:
        kw, vw = [(T.sem.karr, 3 * NE_KV)], [(T.sem.varr, 2 * NE_KV)]
    elif core in rel:
        pcs = [(sy, T.vsb[:, 0:128], T.vs[:], 0), (ac, T.ksb[:], T.ks[:], 1),
               (sy, T.kcb[:, 0:256].bitcast(u8), T.kc[:, 0:1024], 1),
               (ac, T.kcb[:, 256:512].bitcast(u8), T.kc[:, 1024:2048], 1),
               (sy, T.vob[:, 0:128].bitcast(u8), T.vc[:], 0)]
        kw, vw = [], []
        for qu, buf, src, is_k in pcs:
            s_p = new()
            qu.dma_start(buf, src).then_inc(s_p, 16)
            (kw if is_k else vw).append((s_p, 16))
            g.wait_ge(s_p, 16)
            sent += _put(g, T, topo, core, rel[core], buf, buf, T.sem.karr if is_k else T.sem.varr, NE_KV)
    else:
        sy.dma_start(T.kcb[:].bitcast(u8), T.kc[:]).then_inc(s_k, 16)
        ac.dma_start(T.ksb[:], T.ks[:]).then_inc(s_k, 16)
        sy.dma_start(T.vob[:, 0:128].bitcast(u8), T.vc[:]).then_inc(s_v, 16)
        ac.dma_start(T.vsb[:, 0:128], T.vs[:]).then_inc(s_v, 16)
        kw, vw = [(s_k, 32)], [(s_v, 32)]
    dv.wait_ge(s_m, 3)
    if is_root:
        dv.wait_ge(s_q, 16)
        dv.quantize_mx(T.qcb[:], T.qsb[:], T.qt[:]).then_inc(s_qq, 1)

    if is_root:
        off_e = _usable(topo, core, off)[:NE]
        rest = [e for e in _usable(topo, core, on) if e not in off_e]
        on_e = (rest if len(rest) >= NE else _usable(topo, core, on))[:NE]
        g.wait_ge(s_oq, 1)
        sent += _send_one(g, T, topo, leaf, on_e)
        g.wait_ge(s_qq, 1)
        for d in on:
            if d in feeds:
                sent += _send_q(g, T, topo, [d], on_e)
        sent += _send_q(g, T, topo, off, off_e)
        sent += _send_q(g, T, topo, leaf, on_e)
        pe.wait_ge(s_qq, 1)
    else:
        pe.wait_ge(T.sem.qsarr, NE)
        pe.wait_ge(T.sem.qarr, NE)

    ac.wait_ge(s_m, 3)
    ac.activation(T.flo[:], T.m20[:], EXP).then_inc(s_one, 1)
    dv.wait_ge(s_one, 1)

    s_mt = [new() for _ in range(4)]
    s_s = [new() for _ in range(4)]
    for s_p, n_p in kw:
        pe.wait_ge(s_p, n_p)
    for i in range(4):
        pe.matmul_mx(T.ps[:, 512 * i:512 * i + 128], T.qcb[:], T.qsb[:], T.kcb[:, 128 * i:128 * i + 128],
                     T.ksb[:, 128 * i:128 * i + 128], True, True).then_inc(s_mt[i], 1)
    for b in range(4):
        pe.matmul_mx(T.ps[:, 512 * (4 + b):512 * (4 + b) + 128], T.kcb[:, 128 * b:128 * b + 128],
                     T.ksb[:, 128 * b:128 * b + 128], T.qcb[:], T.qsb[:], True, True).then_inc(s_s[b], 1)

    s_r, s_r2, s_y, s_x = new(), new(), new(), new()
    for i in range(4):
        dv.wait_ge(s_mt[i], 1)
        dv.tensor_reduce(T.mr[:, i:i + 1], T.ps[:, 512 * i:512 * i + 128], X, MAX).then_inc(s_r, 1)
    dv.wait_ge(s_r, 4)
    dv.tensor_reduce(T.mr[:, 4:5], T.mr[:, 0:4], X, MAX).then_inc(s_r2, 1)
    dv.wait_ge(s_r2, 1)
    dv.tensor_scalar(T.y[:], T.o32[:], T.mr[:, 4:5], A, MUL, MUL).then_inc(s_y, 1)
    dv.wait_ge(s_y, 1)
    dv.transpose(T.x[:], T.y[:]).then_inc(s_x, 1)
    s_cb = [new() for _ in range(4)]
    g.wait_ge(s_x, 1)
    for a in range(4):
        g.partition_broadcast(T.cb[:, 32 * a:32 * a + 32], T.x[32 * a:32 * a + 1, :], 128).then_inc(s_cb[a], 1)
    s_own = new()
    if is_root:
        dv.tensor_copy(T.cland[:, 4 * rank:4 * rank + 1], T.y[:, 0:1]).then_inc(s_own, 1)
    elif sends:
        sent += _put(g, T, topo, core, root, T.cland[:, 4 * slot:4 * slot + 1], T.y[:, 0:1], T.sem.carr, NE_C)

    s_fl, s_pq, s_a, s_st = new(), new(), new(), new()
    s_t = [new() for _ in range(4)]
    s_sub = [new() for _ in range(4)]
    s_e = [new() for _ in range(4)]
    for b in range(4):
        ac.wait_ge(s_s[b], 1)
        ac.activation(T.t[:, b:512:4], T.ps[:, 512 * (4 + b):512 * (4 + b) + 128], COPY, scale=A).then_inc(s_t[b], 1)

    def floor(a):
        dv.wait_ge(s_e[a], 1)
        dv.tensor_scalar(T.pt[:, 128 * a:128 * a + 128], T.pt[:, 128 * a:128 * a + 128], T.flo[:, 0:1], None,
                         MAX).then_inc(s_fl, 1)

    for a in range(4):
        lo, hi = 128 * a, 128 * a + 128
        dv.wait_ge(s_cb[a], 1)
        for b in range(4):
            if a == 0:
                dv.wait_ge(s_t[b], 1)
            dv.tensor_tensor(T.t[:, lo + b:hi:4], T.t[:, lo + b:hi:4], T.cb[:, 32 * a:32 * a + 32], SUB).then_inc(s_sub[a], 1)
        ac.wait_ge(s_sub[a], 4)
        ac.activation(T.pt[:, lo:hi], T.t[:, lo:hi], EXP).then_inc(s_e[a], 1)
        if a > 0:
            floor(a - 1)
    floor(3)
    dv.wait_ge(s_fl, 4)
    dv.quantize_mx(T.pcb[:], T.psb[:], T.pt[:]).then_inc(s_pq, 1)

    pe.wait_ge(s_pq, 1)
    for s_p, n_p in vw:
        pe.wait_ge(s_p, n_p)
    if maker:
        pe.wait_ge(s_oq, 1)
    else:
        pe.wait_ge(T.sem.oarr, NE)
    pe.matmul_mx(T.ps[:, 0:128 + OW], T.pcb[:], T.psb[:], T.vob[:, 0:128 + OW], T.vsb[:, 0:128 + OW], True,
                 True).then_inc(s_a, 1)
    dv.wait_ge(s_a, 1)
    if is_root:
        dv.tensor_copy(T.land[:, SLOT * rank:SLOT * rank + MSG], T.ps[:, 0:MSG]).then_inc(s_st, 1)
    elif sends:
        dv.tensor_copy(T.st[:, 0:MSG], T.ps[:, 0:MSG]).then_inc(s_st, 1)
        g.wait_ge(s_st, 1)
        sent += _put(g, T, topo, core, root, T.land[:, SLOT * slot:SLOT * slot + MSG], T.st[:, 0:MSG],
                     T.sem["arr%d" % slot], NE_RET)
    if rank is None:
        g.wait_ge(T.sem.lsent, sent)
        return

    s_out = new()
    nout = 0
    if not is_root:
        sy.wait_ge(s_m, 3)
        sy.dma_start(T.w[:], T.zw[0:N, :]).then_inc(s_out, 16)
        nout += 16
    for a in range(4):
        sy.wait_ge(s_cb[a], 1)
    sy.dma_start(T.c[:], T.cb[0:1, :]).then_inc(s_out, 16)
    sy.wait_ge(s_fl, 4)
    if not is_root:
        sy.wait_ge(T.sem.lsent, sent)
    sy.dma_start(T.p[:], T.pt[:]).then_inc(s_out, 16)
    nout += 32

    if not is_root:
        sy.wait_ge(s_out, nout)
        g.wait_ge(T.sem.lsent, sent)
        return

    s_nm, s_w, s_wt = new(), new(), new()
    dv.wait_ge(s_own, 1)
    dv.wait_ge(T.sem.carr, NE_C * (N - 1))
    dv.tensor_reduce(T.nm[:, 0:1], T.cland[:, 0:4 * N:4], X, MAX, negate=True).then_inc(s_nm, 1)
    ac.wait_ge(s_nm, 1)
    ac.wait_ge(s_own, 1)
    ac.wait_ge(T.sem.carr, NE_C * (N - 1))
    ac.activation(T.wt[:, 0:N], T.cland[:, 0:4 * N:4], EXP, bias=T.nm[:, 0:1]).then_inc(s_w, 1)
    ac.wait_ge(s_w, 1)
    dv.wait_ge(s_w, 1)
    dv.transpose(T.wtt[:], T.wt[:]).then_inc(s_wt, 1)
    sy.wait_ge(s_wt, 1)
    for a in range(4):
        sy.dma_start(T.w[:, 32 * a:32 * a + 32], T.wtt[32 * a:32 * a + N, :]).then_inc(s_out, 16)
        nout += 16

    def late(c):
        return (c != root, topo.chip(c) != topo.chip(root), c in fwd, c in rel)
    order = sorted(range(N), key=lambda r: late(cores[r]))
    s_tm = [new() for _ in range(N)]
    s_dn = [new() for _ in range(N)]
    s_ac = [new() for _ in range(N)]
    s_rc, s_f, s_z = new(), new(), new()
    for k, j in enumerate(order):
        if j == rank:
            ac.wait_ge(s_st, 1)
            dv.wait_ge(s_st, 1)
        else:
            ac.wait_ge(T.sem["arr%d" % j], NE_RET)
            dv.wait_ge(T.sem["arr%d" % j], NE_RET)
        ac.activation(T.tm[:, 128 * k:128 * k + 128], T.land[:, SLOT * j:SLOT * j + 128], COPY,
                      scale=T.wt[:, j:j + 1]).then_inc(s_tm[k], 1)
        lcol = T.land[:, SLOT * j + 128:SLOT * j + 129]
        if k == 0:
            dv.tensor_scalar(T.dn[:, 0:1], lcol, T.wt[:, j:j + 1], None, MUL).then_inc(s_dn[0], 1)
        else:
            dv.wait_ge(s_dn[k - 1], 1)
            dv.tensor_scalar(T.dn[:, k:k + 1], lcol, T.wt[:, j:j + 1], T.dn[:, k - 1:k], MUL, ADD).then_inc(s_dn[k], 1)
        if k == N - 1:
            dv.wait_ge(s_dn[k], 1)
            dv.reciprocal(T.rc[:, 0:1], T.dn[:, k:k + 1]).then_inc(s_rc, 1)
        dv.wait_ge(s_tm[k], 1)
        if k == 1:
            dv.tensor_tensor(T.acc[:], T.tm[:, 0:128], T.tm[:, 128:256], ADD).then_inc(s_ac[1], 1)
        elif k == N - 1:
            dv.wait_ge(s_ac[k - 1], 1)
            for b in range(4):
                dv.tensor_tensor(T.ot[:, 32 * b:32 * b + 32], T.acc[:, b:128:4],
                                 T.tm[:, 128 * k + b:128 * k + 128:4], ADD).then_inc(s_ac[k], 1)
        elif k > 1:
            dv.wait_ge(s_ac[k - 1], 1)
            dv.tensor_tensor(T.acc[:], T.acc[:], T.tm[:, 128 * k:128 * k + 128], ADD).then_inc(s_ac[k], 1)

    dv.wait_ge(s_ac[N - 1], 4)
    dv.wait_ge(s_rc, 1)
    ac.wait_ge(s_ac[N - 1], 4)
    ac.wait_ge(s_rc, 1)
    dv.tensor_scalar(T.osc[:, 0:64], T.ot[:, 0:64], T.rc[:, 0:1], None, MUL).then_inc(s_f, 1)
    ac.activation(T.osc[:, 64:128], T.ot[:, 64:128], COPY, scale=T.rc[:, 0:1]).then_inc(s_f, 1)
    dv.wait_ge(s_f, 2)
    dv.transpose(T.z[:], T.osc[:]).then_inc(s_z, 1)
    sy.wait_ge(s_z, 1)
    ac.wait_ge(s_z, 1)
    for a in range(4):
        (sy if a < 2 else ac).dma_start(T.o[:, 32 * a:32 * a + 32], T.z[32 * a:32 * a + 32, :]).then_inc(s_out, 16)
        nout += 16
    sy.wait_ge(s_out, nout)
    g.wait_ge(T.sem.lsent, sent)
